import numpy as np
import ml_dtypes


def mxq(x, axis, fmt="e4m3"):
    dtype, down = {"e4m3": (ml_dtypes.float8_e4m3fn, 7), "e5m2": (ml_dtypes.float8_e5m2, 14)}[fmt]
    v = np.moveaxis(np.asarray(x, np.float32).astype(ml_dtypes.bfloat16).astype(np.float64), axis, -1)
    blocks = v.reshape(v.shape[:-1] + (-1, 32))
    amax = np.abs(blocks).max(-1, keepdims=True)
    byte = np.maximum(np.where(amax > 0, np.frexp(amax)[1] - 1 + 127, 0) - down, 1)
    scale = np.exp2(byte - 127.0)
    codes = (blocks / scale).astype(np.float32).astype(dtype).astype(np.float64)
    return np.moveaxis((codes * scale).reshape(v.shape), -1, axis)


WIDE = False


def mx_kscale(k):
    if not WIDE:
        return np.ones(k)
    levels = np.array([30, -30])
    if k % 512:
        return np.exp2(np.random.permutation(np.resize(levels, k // 32))).repeat(32)
    a = np.empty((k // 512, 16))
    for p in range(k // 512):
        a[p, :8] = np.random.permutation(np.resize(levels, 8))
        for g in range(8):
            far = levels[np.abs(levels - a[p, g]) >= 10]
            a[p, g + 8] = far[np.random.randint(len(far))]
    return np.exp2(a.ravel()).repeat(32)


def f64(x):
    return np.asarray(x).astype(np.float64)


def striped(idx):
    return np.tile(np.asarray(idx).reshape(-1, 16).T, (8, 1)).astype(np.uint16)


def unstriped(offs):
    return offs[:16].T.reshape(-1).astype(np.int64)


E2M1 = np.array([0.0, 0.5, 1.0, 1.5, 2.0, 3.0, 4.0, 6.0, -0.0, -0.5, -1.0, -1.5, -2.0, -3.0, -4.0, -6.0])


def pack_weight(w, fmt):
    k, n = w.shape
    w = f64(np.asarray(w, np.float32).astype(ml_dtypes.bfloat16)).reshape(k // 32, 32, n)
    amax = np.abs(w).max(1)
    if fmt in ("e4m3", "e5m2"):
        byte = np.frexp(amax)[1] - 1 + 127 - (7 if fmt == "e4m3" else 14)
    else:
        mant, ex = np.frexp(amax / 6.0)
        byte = np.where(mant > 0.5, ex, ex - 1) + 127
    byte = np.clip(np.where(amax > 0, byte, 1), 1, 254)
    scaled = (w * np.exp2(127.0 - byte)[:, None, :]).reshape(k, n).astype(np.float32)
    by_word = np.ascontiguousarray(scaled.reshape(k // 512, 128, 4, n).transpose(0, 1, 3, 2))
    if fmt in ("e4m3", "e5m2"):
        words = by_word.astype(ml_dtypes.float8_e4m3fn if fmt == "e4m3" else ml_dtypes.float8_e5m2).view(np.uint8)
    else:
        c = by_word.astype(ml_dtypes.float4_e2m1fn).view(np.uint8) & 0xF
        words = (c[..., 0::2] | (c[..., 1::2] << 4)).reshape(k // 512, 128, 2 * n)
    return np.ascontiguousarray(words), np.ascontiguousarray(byte.astype(np.uint8).reshape(k // 512, 16, n))


def unpack_weight(words, scales, fmt):
    g, _, n = scales.shape
    words = np.ascontiguousarray(words).reshape(g, 128, n, -1)
    if fmt in ("e4m3", "e5m2"):
        vals = words.view(ml_dtypes.float8_e4m3fn if fmt == "e4m3" else ml_dtypes.float8_e5m2).astype(np.float64)
    else:
        nib = np.empty((g, 128, n, 4), np.uint8)
        nib[..., 0::2] = words & 0xF
        nib[..., 1::2] = words >> 4
        vals = E2M1[nib]
    vals = vals * np.repeat(np.exp2(scales.astype(np.float64) - 127.0), 8, axis=1)[..., None]
    return vals.transpose(0, 1, 3, 2).reshape(g * 512, n)


def sgn(shape):
    return np.random.uniform(0.5, 2.0, shape) * np.where(np.random.standard_normal(shape) < 0, -1.0, 1.0)


K, T, J, Q, R, O, N, E = 512, 1024, 256, 128, 512, 128, 256, 256


def setup_inputs():
    n = np.random.standard_normal
    idx = np.random.permutation(T)[:J]
    idx2 = np.random.permutation(J)[:O]
    idx3 = np.random.permutation(J)[:O]
    idx4 = np.random.permutation(J)[:O]
    idx5 = np.random.permutation(J)[:O]
    idx6 = np.random.permutation(E)[:O]
    fk = mx_kscale(K)
    fr = mx_kscale(R)
    xtp = pack_weight(n((K, T)) / fk[:, None], "e2m1")
    wp = pack_weight(n((K, Q)) * 1 / np.sqrt(K) * fk[:, None], "e5m2")
    wbp = pack_weight(n((R, N)) * 1 / np.sqrt(R) / fr[:, None], "e4m3")
    return {
        "xt_words": xtp[0],
        "xt_scales": xtp[1],
        "w_words": wp[0],
        "w_scales": wp[1],
        "sa": (sgn((Q, 1)) * fr[::4, None]).astype(np.float32),
        "sb": (sgn((Q, 1)) * fr[::4, None]).astype(np.float32),
        "sd": (sgn((Q, 1)) * fr[::4, None]).astype(np.float32),
        "se": (sgn((Q, 1)) * fr[::4, None]).astype(np.float32),
        "wb_words": wbp[0],
        "wb_scales": wbp[1],
        "so": (np.random.uniform(0.5, 1.6, (N, 1))).astype(np.float32),
        "offs": striped(idx),
        "offs2": striped(idx2),
        "offs3": striped(idx3),
        "offs4": striped(idx4),
        "offs5": striped(idx5),
        "offs6": striped(idx6),
    }


def reference(xt_words, xt_scales, w_words, w_scales, sa, sb, sd, se, wb_words, wb_scales, so, offs, offs2, offs3, offs4, offs5, offs6):
    idx = unstriped(offs)
    idx2 = unstriped(offs2)
    idx3 = unstriped(offs3)
    idx4 = unstriped(offs4)
    idx5 = unstriped(offs5)
    idx6 = unstriped(offs6)
    xtu = unpack_weight(xt_words, xt_scales, "e2m1")
    wu = unpack_weight(w_words, w_scales, "e5m2")
    wbu = unpack_weight(wb_words, wb_scales, "e4m3")
    xtidxg = xtu[:, idx]
    a = wu.T @ xtidxg
    v0 = a[:, idx2] * f64(sa)
    v1 = a[:, idx3] * f64(sb)
    v2 = a[:, idx4] * f64(sd)
    v3 = a[:, idx5] * f64(se)
    hid = np.stack([v0, v1, v2, v3], axis=1).reshape(R, O)
    hidq = mxq(hid, 0, "e5m2")
    p = wbu.T @ hidq
    y = np.zeros((N, E))
    y[:, idx6] = p * f64(so)
    return y

@@ -1,0 +1,110 @@
+from contextlib import ExitStack
+
+import concourse.mybir as mybir
+
+K, T, J, Q, R, O, N, E = 512, 1024, 256, 128, 512, 128, 256, 256
+FLOPS = 2 * K * Q * J + 2 * R * N * O
+
+F32 = mybir.dt.float32
+BF16 = mybir.dt.bfloat16
+I32 = mybir.dt.int32
+U16 = mybir.dt.uint16
+U8 = mybir.dt.uint8
+E2M1X4 = mybir.dt.float4_e2m1fn_x4
+E5M2X4 = mybir.dt.float8_e5m2_x4
+E4M3X4 = mybir.dt.float8_e4m3fn_x4
+COPY = mybir.ActivationFunctionType.Copy
+
+P = 128
+TAPS = 4
+
+
+def load_quadrant(queue, plane, scales, q):
+    words = scales.shape[2] // 4
+    rows = scales[0, 4 * q : 4 * q + 4, :].bitcast(I32).rearrange("(o r) c -> o r c", o=1)
+    queue.dma_start(out=plane[32 * q : 32 * q + 32, :].bitcast(I32), in_=rows.to_broadcast([8, 4, words]))
+
+
+def load_staged(queue, staged, scales):
+    queue.dma_start(out=staged[0:4, :, :], in_=scales[0].bitcast(I32).rearrange("(q r) c -> r q c", q=4))
+
+
+def spread(nc, plane, staged):
+    for q in range(4):
+        nc.vector.tensor_copy(plane[32 * q : 32 * q + 4, :].bitcast(I32), staged[0:4, q, :])
+
+
+def tile_list_fourtaps_kernel(tc, xt_words, xt_scales, w_words, w_scales, sa, sb, sd, se, wb_words, wb_scales, so,
+                                 offs, offs2, offs3, offs4, offs5, offs6, out):
+    nc = tc.nc
+    with ExitStack() as ctx:
+        keep = ctx.enter_context(tc.tile_pool(name="keep", bufs=1))
+        psum = ctx.enter_context(tc.psum_pool(name="psum", bufs=1))
+
+        tok_list = keep.tile([P, J // 16], U16, name="tok_list")
+        tap_lists = [keep.tile([P, O // 16], U16, name="tap_list%d" % t) for t in range(TAPS)]
+        col_list = keep.tile([P, O // 16], U16, name="col_list")
+        tap_w = [keep.tile([P, 1], F32, name="tap_w%d" % t) for t in range(TAPS)]
+        out_w = keep.tile([P, 2], F32, name="out_w")
+        xt_table = keep.tile([P, T], U16, name="xt_table", align_bytes=64)
+        xt_plane = keep.tile([P, T], U8, name="xt_plane", align_bytes=64)
+        w_codes = keep.tile([P, Q], I32, name="w_codes", align_bytes=64)
+        w_plane = keep.tile([P, Q], U8, name="w_plane", align_bytes=64)
+        wb_codes = keep.tile([P, N], I32, name="wb_codes", align_bytes=64)
+        wb_plane = keep.tile([P, N], U8, name="wb_plane", align_bytes=64)
+
+        w_staged = keep.tile([P, 4, Q // 4], I32, name="w_staged")
+        wb_staged = keep.tile([P, 4, N // 4], I32, name="wb_staged")
+        pages = [keep.tile([P, E], F32, name="page%d" % h) for h in range(2)]
+
+        nc.sync.dma_start(xt_table[:].bitcast(I32), xt_words[0].bitcast(I32))
+        load_staged(nc.scalar, w_staged, w_scales)
+        nc.sync.dma_start(tok_list[:], offs)
+        for q in range(4):
+            load_quadrant(nc.scalar if q % 2 == 0 else nc.sync, xt_plane, xt_scales, q)
+        nc.scalar.dma_start(w_codes[:], w_words[0].rearrange("p n t -> p (n t)").bitcast(I32))
+        for t, (tap_offs, tap_scale) in enumerate(zip((offs2, offs3, offs4, offs5), (sa, sb, sd, se))):
+            nc.sync.dma_start(tap_lists[t][:], tap_offs)
+            nc.sync.dma_start(tap_w[t][:], tap_scale)
+        load_staged(nc.gpsimd, wb_staged, wb_scales)
+        nc.gpsimd.dma_start(wb_codes[:], wb_words[0].rearrange("p n t -> p (n t)").bitcast(I32))
+        nc.sync.dma_start(col_list[:], offs6)
+        with nc.allow_non_contiguous_dma(reason="one weight a partition"):
+            nc.gpsimd.dma_start(out_w[:], so.rearrange("(h p) o -> p (h o)", p=P))
+
+        nc.vector.memset(w_plane[:].bitcast(I32), 0)
+        nc.vector.memset(wb_plane[:].bitcast(I32), 0)
+        for page in pages:
+            nc.vector.memset(page[:], 0.0)
+        spread(nc, w_plane, w_staged)
+
+        picked_plane = keep.tile([P, J], U8, name="picked_plane", align_bytes=64)
+        picked_words = keep.tile([P, J], U16, name="picked_words", align_bytes=64)
+        nc.vector.tensor_copy(picked_words[:], xt_table[:].indirect(tok_list[:]))
+        nc.vector.tensor_copy(picked_plane[:], xt_plane[:].indirect(tok_list[:]))
+
+        a_sum = psum.tile([P, J], F32, name="a_sum")
+        nc.tensor.matmul_mx(out=a_sum[:], lhsT=w_codes[:].bitcast(E5M2X4), lhsT_scale=w_plane[:],
+                            rhs=picked_words[:].bitcast(E2M1X4), rhs_scale=picked_plane[:], start=True, stop=True)
+        a_rows = keep.tile([P, J], F32, name="a_rows")
+        nc.vector.tensor_copy(a_rows[:], a_sum[:])
+
+        spread(nc, wb_plane, wb_staged)
+        hid = keep.tile([P, TAPS * O], BF16, name="hid", align_bytes=64)
+        for t in range(TAPS):
+            nc.scalar.activation(out=hid[:, t : TAPS * O : TAPS], in_=a_rows[:].indirect(tap_lists[t][:]), func=COPY,
+                                 scale=tap_w[t][:])
+        hid_codes = keep.tile([P, O], I32, name="hid_codes", align_bytes=64)
+        hid_plane = keep.tile([P, O], U8, name="hid_plane", align_bytes=64)
+        nc.vector.quantize_mx(out=hid_codes[:].bitcast(E5M2X4), scales=hid_plane[:], in_=hid[:])
+
+        for h in range(2):
+            cols = slice(h * P, (h + 1) * P)
+            p_sum = psum.tile([P, O], F32, name="p_sum%d" % h)
+            nc.tensor.matmul_mx(out=p_sum[:], lhsT=wb_codes[:, cols].bitcast(E4M3X4), lhsT_scale=wb_plane[:, cols],
+                                rhs=hid_codes[:].bitcast(E5M2X4), rhs_scale=hid_plane[:], start=True, stop=True)
+            p_rows = keep.tile([P, O], F32, name="p_rows%d" % h)
+            nc.vector.tensor_copy(p_rows[:], p_sum[:])
+            nc.scalar.activation(out=pages[h][:].indirect(col_list[:]), in_=p_rows[:], func=COPY,
+                                 scale=out_w[:, h : h + 1])
+            nc.sync.dma_start(out[cols, :], pages[h][:])

@@ -47,18 +47,17 @@ def tile_list_fourtaps_kernel(tc, xt_words, xt_scales, w_words, w_scales, sa, sb
         tap_w = [keep.tile([P, 1], F32, name="tap_w%d" % t) for t in range(TAPS)]
         out_w = keep.tile([P, 2], F32, name="out_w")
         xt_table = keep.tile([P, T], U16, name="xt_table", align_bytes=64)
-        xt_plane = keep.tile([P, T], U8, name="xt_plane", align_bytes=64)
+        xt_plane = keep.tile([P, T], U8, name="xt_plane", tag="plane", align_bytes=64)
         w_codes = keep.tile([P, Q], I32, name="w_codes", align_bytes=64)
         w_plane = keep.tile([P, Q], U8, name="w_plane", align_bytes=64)
         wb_codes = keep.tile([P, N], I32, name="wb_codes", align_bytes=64)
-        wb_plane = keep.tile([P, N], U8, name="wb_plane", align_bytes=64)
 
         w_staged = keep.tile([P, 4, Q // 4], I32, name="w_staged")
         wb_staged = keep.tile([P, 4, N // 4], I32, name="wb_staged")
         pages = [keep.tile([P, E], F32, name="page%d" % h) for h in range(2)]
 
-        nc.sync.dma_start(xt_table[:].bitcast(I32), xt_words[0].bitcast(I32))
         load_staged(nc.scalar, w_staged, w_scales)
+        nc.sync.dma_start(xt_table[:].bitcast(I32), xt_words[0].bitcast(I32))
         nc.sync.dma_start(tok_list[:], offs)
         for q in range(4):
             load_quadrant(nc.scalar if q % 2 == 0 else nc.sync, xt_plane, xt_scales, q)
@@ -73,7 +72,6 @@ def tile_list_fourtaps_kernel(tc, xt_words, xt_scales, w_words, w_scales, sa, sb
             nc.gpsimd.dma_start(out_w[:], so.rearrange("(h p) o -> p (h o)", p=P))
 
         nc.vector.memset(w_plane[:].bitcast(I32), 0)
-        nc.vector.memset(wb_plane[:].bitcast(I32), 0)
         for page in pages:
             nc.vector.memset(page[:], 0.0)
         spread(nc, w_plane, w_staged)
@@ -81,14 +79,18 @@ def tile_list_fourtaps_kernel(tc, xt_words, xt_scales, w_words, w_scales, sa, sb
         picked_plane = keep.tile([P, J], U8, name="picked_plane", align_bytes=64)
         picked_words = keep.tile([P, J], U16, name="picked_words", align_bytes=64)
         nc.vector.tensor_copy(picked_words[:], xt_table[:].indirect(tok_list[:]))
-        nc.vector.tensor_copy(picked_plane[:], xt_plane[:].indirect(tok_list[:]))
-
-        a_sum = psum.tile([P, J], F32, name="a_sum")
-        nc.tensor.matmul_mx(out=a_sum[:], lhsT=w_codes[:].bitcast(E5M2X4), lhsT_scale=w_plane[:],
-                            rhs=picked_words[:].bitcast(E2M1X4), rhs_scale=picked_plane[:], start=True, stop=True)
         a_rows = keep.tile([P, J], F32, name="a_rows")
-        nc.vector.tensor_copy(a_rows[:], a_sum[:])
+        for h in range(2):
+            slots = slice(h * P, (h + 1) * P)
+            nc.vector.tensor_copy(picked_plane[:, slots], xt_plane[:].indirect(tok_list[:, h * 8 : (h + 1) * 8]))
+            a_sum = psum.tile([P, P], F32, name="a_sum%d" % h)
+            nc.tensor.matmul_mx(out=a_sum[:], lhsT=w_codes[:].bitcast(E5M2X4), lhsT_scale=w_plane[:],
+                                rhs=picked_words[:, slots].bitcast(E2M1X4), rhs_scale=picked_plane[:, slots],
+                                start=True, stop=True)
+            nc.scalar.activation(out=a_rows[:, slots], in_=a_sum[:], func=COPY)
 
+        wb_plane = keep.tile([P, N], U8, name="wb_plane", tag="plane", align_bytes=64)
+        nc.vector.memset(wb_plane[:].bitcast(I32), 0)
         spread(nc, wb_plane, wb_staged)
         hid = keep.tile([P, TAPS * O], BF16, name="hid", align_bytes=64)
         for t in range(TAPS):

@@ -20,9 +20,7 @@ TAPS = 4
 
 
 def load_quadrant(queue, plane, scales, q):
-    words = scales.shape[2] // 4
-    rows = scales[0, 4 * q : 4 * q + 4, :].bitcast(I32).rearrange("(o r) c -> o r c", o=1)
-    queue.dma_start(out=plane[32 * q : 32 * q + 32, :].bitcast(I32), in_=rows.to_broadcast([8, 4, words]))
+    queue.dma_start(out=plane[32 * q : 32 * q + 4, :].bitcast(I32), in_=scales[0, 4 * q : 4 * q + 4, :].bitcast(I32))
 
 
 def load_staged(queue, staged, scales):
@@ -56,20 +54,21 @@ def tile_list_fourtaps_kernel(tc, xt_words, xt_scales, w_words, w_scales, sa, sb
         wb_staged = keep.tile([P, 4, N // 4], I32, name="wb_staged")
         pages = [keep.tile([P, E], F32, name="page%d" % h) for h in range(2)]
 
+        nc.vector.memset(xt_plane[:].bitcast(I32), 0)
         load_staged(nc.scalar, w_staged, w_scales)
         nc.sync.dma_start(xt_table[:].bitcast(I32), xt_words[0].bitcast(I32))
         nc.sync.dma_start(tok_list[:], offs)
+        nc.scalar.dma_start(w_codes[:], w_words[0].rearrange("p n t -> p (n t)").bitcast(I32))
         for q in range(4):
             load_quadrant(nc.scalar if q % 2 == 0 else nc.sync, xt_plane, xt_scales, q)
-        nc.scalar.dma_start(w_codes[:], w_words[0].rearrange("p n t -> p (n t)").bitcast(I32))
         for t, (tap_offs, tap_scale) in enumerate(zip((offs2, offs3, offs4, offs5), (sa, sb, sd, se))):
             nc.sync.dma_start(tap_lists[t][:], tap_offs)
             nc.sync.dma_start(tap_w[t][:], tap_scale)
-        load_staged(nc.gpsimd, wb_staged, wb_scales)
-        nc.gpsimd.dma_start(wb_codes[:], wb_words[0].rearrange("p n t -> p (n t)").bitcast(I32))
+        load_staged(nc.sync, wb_staged, wb_scales)
+        nc.sync.dma_start(wb_codes[:], wb_words[0].rearrange("p n t -> p (n t)").bitcast(I32))
         nc.sync.dma_start(col_list[:], offs6)
         with nc.allow_non_contiguous_dma(reason="one weight a partition"):
-            nc.gpsimd.dma_start(out_w[:], so.rearrange("(h p) o -> p (h o)", p=P))
+            nc.sync.dma_start(out_w[:], so.rearrange("(h p) o -> p (h o)", p=P))
 
         nc.vector.memset(w_plane[:].bitcast(I32), 0)
         for page in pages:

@@ -55,22 +55,21 @@ def tile_list_fourtaps_kernel(tc, xt_words, xt_scales, w_words, w_scales, sa, sb
         pages = [keep.tile([P, E], F32, name="page%d" % h) for h in range(2)]
 
         nc.vector.memset(xt_plane[:].bitcast(I32), 0)
-        load_staged(nc.scalar, w_staged, w_scales)
-        nc.sync.dma_start(xt_table[:].bitcast(I32), xt_words[0].bitcast(I32))
+        load_staged(nc.sync, w_staged, w_scales)
+        nc.scalar.dma_start(xt_table[:].bitcast(I32), xt_words[0].bitcast(I32))
         nc.sync.dma_start(tok_list[:], offs)
         nc.scalar.dma_start(w_codes[:], w_words[0].rearrange("p n t -> p (n t)").bitcast(I32))
         for q in range(4):
             load_quadrant(nc.scalar if q % 2 == 0 else nc.sync, xt_plane, xt_scales, q)
         for t, (tap_offs, tap_scale) in enumerate(zip((offs2, offs3, offs4, offs5), (sa, sb, sd, se))):
             nc.sync.dma_start(tap_lists[t][:], tap_offs)
-            nc.sync.dma_start(tap_w[t][:], tap_scale)
-        load_staged(nc.sync, wb_staged, wb_scales)
-        nc.sync.dma_start(wb_codes[:], wb_words[0].rearrange("p n t -> p (n t)").bitcast(I32))
+            (nc.gpsimd if t == 0 else nc.sync).dma_start(tap_w[t][:], tap_scale)
+        load_staged(nc.gpsimd, wb_staged, wb_scales)
+        nc.gpsimd.dma_start(wb_codes[:], wb_words[0].rearrange("p n t -> p (n t)").bitcast(I32))
         nc.sync.dma_start(col_list[:], offs6)
         with nc.allow_non_contiguous_dma(reason="one weight a partition"):
             nc.sync.dma_start(out_w[:], so.rearrange("(h p) o -> p (h o)", p=P))
 
-        nc.vector.memset(w_plane[:].bitcast(I32), 0)
         for page in pages:
             nc.vector.memset(page[:], 0.0)
         spread(nc, w_plane, w_staged)
@@ -89,7 +88,6 @@ def tile_list_fourtaps_kernel(tc, xt_words, xt_scales, w_words, w_scales, sa, sb
             nc.scalar.activation(out=a_rows[:, slots], in_=a_sum[:], func=COPY)
 
         wb_plane = keep.tile([P, N], U8, name="wb_plane", tag="plane", align_bytes=64)
-        nc.vector.memset(wb_plane[:].bitcast(I32), 0)
         spread(nc, wb_plane, wb_staged)
         hid = keep.tile([P, TAPS * O], BF16, name="hid", align_bytes=64)
         for t in range(TAPS):

from contextlib import ExitStack

import concourse.mybir as mybir

K, T, J, Q, R, O, N, E = 512, 1024, 256, 128, 512, 128, 256, 256
FLOPS = 2 * K * Q * J + 2 * R * N * O

F32 = mybir.dt.float32
BF16 = mybir.dt.bfloat16
I32 = mybir.dt.int32
U16 = mybir.dt.uint16
U8 = mybir.dt.uint8
E2M1X4 = mybir.dt.float4_e2m1fn_x4
E5M2X4 = mybir.dt.float8_e5m2_x4
E4M3X4 = mybir.dt.float8_e4m3fn_x4
COPY = mybir.ActivationFunctionType.Copy

P = 128
TAPS = 4


def load_quadrant(queue, plane, scales, q):
    queue.dma_start(out=plane[32 * q : 32 * q + 4, :].bitcast(I32), in_=scales[0, 4 * q : 4 * q + 4, :].bitcast(I32))


def load_staged(queue, staged, scales):
    queue.dma_start(out=staged[0:4, :, :], in_=scales[0].bitcast(I32).rearrange("(q r) c -> r q c", q=4))


def spread(nc, plane, staged):
    for q in range(4):
        nc.vector.tensor_copy(plane[32 * q : 32 * q + 4, :].bitcast(I32), staged[0:4, q, :])


def tile_list_fourtaps_kernel(tc, xt_words, xt_scales, w_words, w_scales, sa, sb, sd, se, wb_words, wb_scales, so,
                                 offs, offs2, offs3, offs4, offs5, offs6, out):
    nc = tc.nc
    with ExitStack() as ctx:
        keep = ctx.enter_context(tc.tile_pool(name="keep", bufs=1))
        psum = ctx.enter_context(tc.psum_pool(name="psum", bufs=1))

        tok_list = keep.tile([P, J // 16], U16, name="tok_list")
        tap_lists = [keep.tile([P, O // 16], U16, name="tap_list%d" % t) for t in range(TAPS)]
        col_list = keep.tile([P, O // 16], U16, name="col_list")
        tap_w = [keep.tile([P, 1], F32, name="tap_w%d" % t) for t in range(TAPS)]
        out_w = keep.tile([P, 2], F32, name="out_w")
        xt_table = keep.tile([P, T], U16, name="xt_table", align_bytes=64)
        xt_plane = keep.tile([P, T], U8, name="xt_plane", tag="plane", align_bytes=64)
        w_codes = keep.tile([P, Q], I32, name="w_codes", align_bytes=64)
        w_plane = keep.tile([P, Q], U8, name="w_plane", align_bytes=64)
        wb_codes = keep.tile([P, N], I32, name="wb_codes", align_bytes=64)

        w_staged = keep.tile([P, 4, Q // 4], I32, name="w_staged")
        wb_staged = keep.tile([P, 4, N // 4], I32, name="wb_staged")
        pages = [keep.tile([P, E], F32, name="page%d" % h) for h in range(2)]

        nc.vector.memset(xt_plane[:].bitcast(I32), 0)
        load_staged(nc.sync, w_staged, w_scales)
        nc.scalar.dma_start(xt_table[:].bitcast(I32), xt_words[0].bitcast(I32))
        nc.sync.dma_start(tok_list[:], offs)
        nc.scalar.dma_start(w_codes[:], w_words[0].rearrange("p n t -> p (n t)").bitcast(I32))
        for q in range(4):
            load_quadrant(nc.scalar if q % 2 == 0 else nc.sync, xt_plane, xt_scales, q)
        for t, (tap_offs, tap_scale) in enumerate(zip((offs2, offs3, offs4, offs5), (sa, sb, sd, se))):
            nc.sync.dma_start(tap_lists[t][:], tap_offs)
            (nc.gpsimd if t == 0 else nc.sync).dma_start(tap_w[t][:], tap_scale)
        load_staged(nc.gpsimd, wb_staged, wb_scales)
        nc.gpsimd.dma_start(wb_codes[:], wb_words[0].rearrange("p n t -> p (n t)").bitcast(I32))
        nc.sync.dma_start(col_list[:], offs6)
        with nc.allow_non_contiguous_dma(reason="one weight a partition"):
            nc.sync.dma_start(out_w[:], so.rearrange("(h p) o -> p (h o)", p=P))

        for page in pages:
            nc.vector.memset(page[:], 0.0)
        spread(nc, w_plane, w_staged)

        picked_plane = keep.tile([P, J], U8, name="picked_plane", align_bytes=64)
        picked_words = keep.tile([P, J], U16, name="picked_words", align_bytes=64)
        nc.vector.tensor_copy(picked_words[:], xt_table[:].indirect(tok_list[:]))
        a_rows = keep.tile([P, J], F32, name="a_rows")
        for h in range(2):
            slots = slice(h * P, (h + 1) * P)
            nc.vector.tensor_copy(picked_plane[:, slots], xt_plane[:].indirect(tok_list[:, h * 8 : (h + 1) * 8]))
            a_sum = psum.tile([P, P], F32, name="a_sum%d" % h)
            nc.tensor.matmul_mx(out=a_sum[:], lhsT=w_codes[:].bitcast(E5M2X4), lhsT_scale=w_plane[:],
                                rhs=picked_words[:, slots].bitcast(E2M1X4), rhs_scale=picked_plane[:, slots],
                                start=True, stop=True)
            nc.scalar.activation(out=a_rows[:, slots], in_=a_sum[:], func=COPY)

        wb_plane = keep.tile([P, N], U8, name="wb_plane", tag="plane", align_bytes=64)
        spread(nc, wb_plane, wb_staged)
        hid = keep.tile([P, TAPS * O], BF16, name="hid", align_bytes=64)
        for t in range(TAPS):
            nc.scalar.activation(out=hid[:, t : TAPS * O : TAPS], in_=a_rows[:].indirect(tap_lists[t][:]), func=COPY,
                                 scale=tap_w[t][:])
        hid_codes = keep.tile([P, O], I32, name="hid_codes", align_bytes=64)
        hid_plane = keep.tile([P, O], U8, name="hid_plane", align_bytes=64)
        nc.vector.quantize_mx(out=hid_codes[:].bitcast(E5M2X4), scales=hid_plane[:], in_=hid[:])

        for h in range(2):
            cols = slice(h * P, (h + 1) * P)
            p_sum = psum.tile([P, O], F32, name="p_sum%d" % h)
            nc.tensor.matmul_mx(out=p_sum[:], lhsT=wb_codes[:, cols].bitcast(E4M3X4), lhsT_scale=wb_plane[:, cols],
                                rhs=hid_codes[:].bitcast(E5M2X4), rhs_scale=hid_plane[:], start=True, stop=True)
            p_rows = keep.tile([P, O], F32, name="p_rows%d" % h)
            nc.vector.tensor_copy(p_rows[:], p_sum[:])
            nc.scalar.activation(out=pages[h][:].indirect(col_list[:]), in_=p_rows[:], func=COPY,
                                 scale=out_w[:, h : h + 1])
            nc.sync.dma_start(out[cols, :], pages[h][:])
